import numpy as np
import ml_dtypes


def mxq(x, axis, fmt="e4m3"):
    dtype, down = {"e4m3": (ml_dtypes.float8_e4m3fn, 7), "e5m2": (ml_dtypes.float8_e5m2, 14)}[fmt]
    v = np.moveaxis(np.asarray(x, np.float32).astype(ml_dtypes.bfloat16).astype(np.float64), axis, -1)
    blocks = v.reshape(v.shape[:-1] + (-1, 32))
    amax = np.abs(blocks).max(-1, keepdims=True)
    byte = np.maximum(np.where(amax > 0, np.frexp(amax)[1] - 1 + 127, 0) - down, 1)
    scale = np.exp2(byte - 127.0)
    codes = (blocks / scale).astype(np.float32).astype(dtype).astype(np.float64)
    return np.moveaxis((codes * scale).reshape(v.shape), -1, axis)


WIDE = False


def mx_kscale(k):
    if not WIDE:
        return np.ones(k)
    levels = np.array([10, -10, 5, -5, 0])
    if k % 512:
        return np.exp2(np.random.permutation(np.resize(levels, k // 32))).repeat(32)
    a = np.empty((k // 512, 16))
    for p in range(k // 512):
        a[p, :8] = np.random.permutation(np.resize(levels, 8))
        for g in range(8):
            far = levels[np.abs(levels - a[p, g]) >= 10]
            a[p, g + 8] = far[np.random.randint(len(far))]
    return np.exp2(a.ravel()).repeat(32)


def f64(x):
    return np.asarray(x).astype(np.float64)


def striped(idx):
    return np.tile(idx.reshape(-1, 16).T, (8, 1)).astype(np.uint16)


def unstriped(offs):
    return offs[:16].T.reshape(-1).astype(np.int64)


def striped8(idx):
    return np.concatenate([x.reshape(-1, 16).T for x in idx]).astype(np.uint16)


def runs(offs, k):
    lists = np.stack([offs[16 * r : 16 * r + 16].T.reshape(-1) for r in range(8)]).astype(np.int64)
    return lists[np.arange(k) % 512 // 64]


def pack_weight(w):
    k, n = w.shape
    w = f64(np.asarray(w, np.float32).astype(ml_dtypes.bfloat16)).reshape(k // 32, 32, n)
    amax = np.abs(w).max(1)
    byte = np.clip(np.where(amax > 0, np.frexp(amax)[1] - 1 + 127 - 7, 1), 1, 254)
    scaled = (w * np.exp2(127.0 - byte)[:, None, :]).reshape(k, n).astype(np.float32)
    words = np.ascontiguousarray(scaled.reshape(k // 512, 128, 4, n).transpose(0, 1, 3, 2)).astype(ml_dtypes.float8_e4m3fn).view(np.uint8)
    return words, np.ascontiguousarray(byte.astype(np.uint8).reshape(k // 512, 16, n))


def unpack_weight(words, scales):
    g, p, n, _ = words.shape
    vals = np.ascontiguousarray(words).view(ml_dtypes.float8_e4m3fn).astype(np.float64) * np.repeat(np.exp2(scales.astype(np.float64) - 127.0), 8, axis=1)[..., None]
    return vals.transpose(0, 1, 3, 2).reshape(g * 512, n)


E2M1 = np.array([0.0, 0.5, 1.0, 1.5, 2.0, 3.0, 4.0, 6.0, -0.0, -0.5, -1.0, -1.5, -2.0, -3.0, -4.0, -6.0])


def pack_fp4(w):
    k, n = w.shape
    w = f64(np.asarray(w, np.float32).astype(ml_dtypes.bfloat16)).reshape(k // 32, 32, n)
    amax = np.abs(w).max(1)
    mant, ex = np.frexp(amax / 6.0)
    byte = np.clip(np.where(amax > 0, np.where(mant > 0.5, ex, ex - 1) + 127, 1), 1, 254)
    scaled = (w * np.exp2(127.0 - byte)[:, None, :]).reshape(k, n).astype(np.float32)
    c = np.ascontiguousarray(scaled.reshape(k // 512, 128, 4, n).transpose(0, 1, 3, 2)).astype(ml_dtypes.float4_e2m1fn).view(np.uint8) & 0xF
    words = (c[..., 0::2] | (c[..., 1::2] << 4)).reshape(k // 512, 128, 2 * n)
    return np.ascontiguousarray(words), np.ascontiguousarray(byte.astype(np.uint8).reshape(k // 512, 16, n))


def unpack_fp4(words, scales):
    g, _, n = scales.shape
    words = np.ascontiguousarray(words).reshape(g, 128, n, 2)
    nib = np.empty((g, 128, n, 4), np.uint8)
    nib[..., 0::2] = words & 0xF
    nib[..., 1::2] = words >> 4
    vals = E2M1[nib] * np.repeat(np.exp2(scales.astype(np.float64) - 127.0), 8, axis=1)[..., None]
    return vals.transpose(0, 1, 3, 2).reshape(g * 512, n)


K, T, S, N, G, H, W = 512, 1024, 512, 512, 2048, 512, 256


def setup_inputs():
    n = np.random.standard_normal
    s = mx_kscale(K)[:, None]
    u = mx_kscale(S)
    packed_xT = pack_weight(n((K, T)) * s)
    packed_dT = pack_weight(n((K, G)) / s)
    packed_w1 = pack_fp4(n((H, N)) / np.sqrt(H) / u[:, None])
    perm = np.random.permutation(S)
    perm2 = np.random.permutation(S)
    return {
        "x_words": packed_xT[0],
        "x_scales": packed_xT[1],
        "d_words": packed_dT[0],
        "d_scales": packed_dT[1],
        "gn": (np.random.uniform(0.5, 1.5, (H, 1)) * u[:, None]).astype(np.float32),
        "w1_words": packed_w1[0],
        "w1_scales": packed_w1[1],
        "offs": striped(np.random.permutation(T)[:S]),
        "k1": striped8(np.random.randint(0, G, (8, H))),
        "hz": striped8(np.random.randint(0, T, (8, S))),
        "k2": striped8(np.random.randint(0, G, (8, H))),
        "n1": striped(perm[:W]),
        "n2": striped(perm[W:]),
        "n3": striped(perm2[:W]),
        "n4": striped(perm2[W:]),
        "n5": striped(np.random.permutation(S)),
        "n6": striped(np.random.permutation(S)),
        "n7": striped(np.random.permutation(S)),
    }


def reference(x_words, x_scales, d_words, d_scales, gn, w1_words, w1_scales, offs, k1, hz, k2, n1, n2, n3, n4, n5, n6, n7):
    d_k1 = unpack_weight(d_words, d_scales)[np.arange(K)[:, None], runs(k1, K)]
    xq = unpack_weight(x_words, x_scales)[:, unstriped(offs)]
    d_k2 = unpack_weight(d_words, d_scales)[np.arange(K)[:, None], runs(k2, K)]
    x_hz = unpack_weight(x_words, x_scales)[np.arange(K)[:, None], runs(hz, K)]
    h = 0.0625 * (d_k1.T @ xq + d_k2.T @ x_hz)
    pa = h[:, unstriped(n1)]
    pb = h[:, unstriped(n2)]
    rb = np.maximum(pa, pb)
    ua = np.zeros((H, S))
    ua[:, unstriped(n3)] = pb
    ub = ua.copy()
    ub[:, unstriped(n4)] = rb
    z = f64(gn) * (ub - h[:, unstriped(n5)])
    h2 = unpack_fp4(w1_words, w1_scales).T @ mxq(z, 0, "e4m3")
    ds = np.zeros((N, S))
    ds[:, unstriped(n6)] = h2
    ds2 = np.zeros((N, S))
    ds2[:, unstriped(n7)] = h2
    return np.maximum(ds, ds2)

@@ -1,0 +1,259 @@
+from contextlib import ExitStack
+
+import concourse.mybir as mybir
+from concourse.masks import make_identity
+
+F32 = mybir.dt.float32
+BF16 = mybir.dt.bfloat16
+I32 = mybir.dt.int32
+U32 = mybir.dt.uint32
+U16 = mybir.dt.uint16
+U8 = mybir.dt.uint8
+FP8X4 = mybir.dt.float8_e4m3fn_x4
+FP4X4 = mybir.dt.float4_e2m1fn_x4
+ALU = mybir.AluOpType
+COPY = mybir.ActivationFunctionType.Copy
+
+P = 128
+PACK = 4
+T, G, S, W = 1024, 2048, 512, 256
+EARLY = 128
+LATE = S - EARLY
+FLOPS = 3 * 2 * 512 * 512 * 512
+
+
+def tile_picked_mthzncpswsendtwo_none_p_kernel(
+    tc, x_words, x_scales, d_words, d_scales, gn, w1_words, w1_scales,
+    offs, k1, hz, k2, n1, n2, n3, n4, n5, n6, n7, out,
+):
+    nc = tc.nc
+    with ExitStack() as ctx:
+        keep = ctx.enter_context(tc.tile_pool(name="keep", bufs=1))
+        psum = ctx.enter_context(tc.psum_pool(name="psum", bufs=1))
+
+        def load_list(ap, name):
+            tile = keep.tile(list(ap.shape), U16, name=name)
+            nc.sync.dma_start(tile[:], ap)
+            return tile
+
+        def load_scale_table(ap, cols, name):
+            tile = keep.tile([P, cols], U8, name=name, align_bytes=64)
+            rows = ap[0].bitcast(I32).unsqueeze(1).to_broadcast([16, 8, cols // 4])
+            nc.sync.dma_start(tile[:].bitcast(I32), rows)
+            return tile
+
+        def load_word_table(ap, cols, name):
+            tile = keep.tile([P, cols], I32, name=name, tag=name, align_bytes=64)
+            nc.sync.dma_start(tile[:], ap[0].rearrange("p n t -> p (n t)").bitcast(I32))
+            return tile
+
+        l_offs = load_list(offs, "l_offs")
+        xs_table = load_scale_table(x_scales, T, "xs_table")
+        l_hz = load_list(hz, "l_hz")
+        ds_table = load_scale_table(d_scales, G, "ds_table")
+        l_k1 = load_list(k1, "l_k1")
+        l_k2 = load_list(k2, "l_k2")
+        dw_table = load_word_table(d_words, G, "dw_table")
+        xw_table = load_word_table(x_words, T, "xw_table")
+        l_n1 = load_list(n1, "l_n1")
+        l_n2 = load_list(n2, "l_n2")
+        l_n5 = load_list(n5, "l_n5")
+        l_n3 = load_list(n3, "l_n3")
+        l_n4 = load_list(n4, "l_n4")
+        l_n6 = load_list(n6, "l_n6")
+        l_n7 = load_list(n7, "l_n7")
+        gain = keep.tile([P, PACK], F32, name="gain")
+        with nc.allow_non_contiguous_dma(reason="one gain a partition and tile"):
+            nc.sync.dma_start(gain[:], gn.rearrange("(a p) o -> p (a o)", p=P))
+        ident_bf = keep.tile([P, P], BF16, name="ident_bf")
+        make_identity(nc, ident_bf[:])
+        ident_f32 = keep.tile([P, P], F32, name="ident_f32")
+        make_identity(nc, ident_f32[:])
+
+        def bank(n, shape, dtype, name):
+            return psum.tile(shape, dtype, name=name, tag=f"bank{n}")
+
+        def place_scale_rows(picked, cols, name):
+            plane = keep.tile([P, cols], U8, name=name, tag=name, align_bytes=64)
+            nc.vector.memset(plane[:].bitcast(I32), 0)
+            for q in range(4):
+                nc.sync.dma_start(plane[32 * q : 32 * q + 4, :].bitcast(I32), picked[32 * q : 32 * q + 32 : 8, :].bitcast(I32))
+            return plane
+
+        def half(lst, c):
+            return lst[:, c * (W // 16) : (c + 1) * (W // 16)]
+
+        bytes_first = keep.tile([P, 3 * S], U8, name="bytes_first", tag="bytes_first", align_bytes=64)
+        for u, lst in enumerate((l_offs, l_hz)):
+            nc.vector.tensor_copy(bytes_first[:, u * S : (u + 1) * S], xs_table[:].indirect(lst[:]))
+        for u, lst in enumerate((l_k1, l_k2)):
+            nc.vector.tensor_copy(bytes_first[:, 2 * S + u * W : 2 * S + (u + 1) * W], ds_table[:].indirect(half(lst, 0)))
+        planes_first = place_scale_rows(bytes_first, 3 * S, "planes_first")
+
+        d_first = keep.tile([P, S], U32, name="d_first", align_bytes=64)
+        x_picked = keep.tile([P, 2 * S], U32, name="x_picked", align_bytes=64)
+        for u, lst in enumerate((l_k1, l_k2)):
+            nc.vector.tensor_copy(d_first[:, u * W : (u + 1) * W], dw_table[:].bitcast(U32).indirect(half(lst, 0)))
+        nc.vector.tensor_copy(x_picked[:, :S], xw_table[:].bitcast(U32).indirect(l_offs[:]))
+        for c in range(2):
+            nc.vector.tensor_copy(x_picked[:, S + c * W : S + (c + 1) * W], xw_table[:].bitcast(U32).indirect(half(l_hz, c)))
+
+        bytes_second = keep.tile([P, S], U8, name="bytes_second", tag="xw_table", align_bytes=64)
+        for u, lst in enumerate((l_k1, l_k2)):
+            nc.vector.tensor_copy(bytes_second[:, u * W : (u + 1) * W], ds_table[:].indirect(half(lst, 1)))
+        planes_second = place_scale_rows(bytes_second, S, "planes_second")
+        w1_codes = keep.tile([P, 2 * S], U8, name="w1_codes", tag="bytes_first", align_bytes=64)
+        nc.sync.dma_start(w1_codes[:].bitcast(I32), w1_words[0].bitcast(I32))
+        w1_plane = keep.tile([P, S], U8, name="w1_plane", tag="xw_table", align_bytes=64)
+        nc.gpsimd.memset(w1_plane[:].bitcast(I32), 0)
+        for q in range(4):
+            nc.sync.dma_start(w1_plane[32 * q : 32 * q + 4, :].bitcast(I32), w1_scales[0, 4 * q : 4 * q + 4, :].bitcast(I32))
+
+        def first_product(acc, d_codes, d_plane, a, c0, c1):
+            for u in range(2):
+                m0 = u * W + (a % 2) * P
+                nc.tensor.matmul_mx(
+                    out=acc,
+                    lhsT=d_codes[:, m0 : m0 + P].bitcast(FP8X4),
+                    lhsT_scale=d_plane[:, m0 : m0 + P],
+                    rhs=x_picked[:, u * S + c0 : u * S + c1].bitcast(FP8X4),
+                    rhs_scale=planes_first[:, u * S + c0 : u * S + c1],
+                    start=(u == 0),
+                    stop=(u == 1),
+                )
+
+        def early_z(a, z):
+            nc.vector.scalar_tensor_tensor(z, ubg_tiles[a][:, :EARLY], gain[:, a : a + 1], h5g_tiles[a][:], ALU.mult, ALU.subtract)
+            turned = bank(3, [P, P], BF16, f"turned_early{a}")
+            nc.tensor.transpose(turned[:], z, ident_bf[:])
+            nc.vector.tensor_copy(zt_early[:, a * P : (a + 1) * P], turned[:])
+
+        def late_gained(a, ubg):
+            nc.vector.tensor_scalar(ubg, ubg_tiles[a][:, EARLY:], gain[:, a : a + 1], None, ALU.mult)
+            gained.append(ubg)
+
+        h5g_tiles, gained = [], []
+        neg_gain = keep.tile([P, PACK], F32, name="neg_gain")
+        zt_early = keep.tile([P, S], BF16, name="zt_early", align_bytes=64)
+        zt_late = keep.tile([P, 3, S], BF16, name="zt_late", align_bytes=64)
+        h_tiles, ubg_tiles = [], []
+        d_codes, d_plane = d_first, planes_first[:, 2 * S :]
+        for a in range(PACK):
+            h = keep.tile([P, S], F32, name=f"h{a}", tag="pa0" if a == 1 else f"h{a}", align_bytes=64)
+            if a == 0:
+                for c in range(2):
+                    acc = bank(c, [P, W], F32, f"acc0_{c}")
+                    first_product(acc[:], d_codes, d_plane, a, c * W, (c + 1) * W)
+                    nc.scalar.activation(h[:, c * W : (c + 1) * W], acc[:], COPY, scale=0.0625)
+            else:
+                acc = bank((a + 1) % 3, [P, S], F32, f"acc{a}")
+                first_product(acc[:], d_codes, d_plane, a, 0, S)
+                nc.vector.tensor_scalar(h[:], acc[:], 0.0625, None, ALU.mult)
+            h_tiles.append(h)
+
+            pa = keep.tile([P, W], F32, name=f"pa{a}", tag=f"pa{a}", align_bytes=64)
+            pb = keep.tile([P, W], F32, name=f"pb{a}")
+            h5 = keep.tile([P, EARLY], F32, name=f"h5_early{a}", tag=f"h5_early{a}", align_bytes=64)
+            h5g = keep.tile([P, EARLY], F32, name=f"h5g_early{a}", tag="planes_second" if a == 1 else f"h5g_early{a}", align_bytes=64)
+            ub = keep.tile([P, S], F32, name=f"ub{a}")
+            nc.vector.tensor_copy(pb[:], h[:].indirect(l_n2[:]))
+            if a == 1:
+                d_second = keep.tile([P, S], U32, name="d_second", tag="h5_early0", align_bytes=64)
+                for u, lst in enumerate((l_k1, l_k2)):
+                    nc.vector.tensor_copy(d_second[:, u * W : (u + 1) * W], dw_table[:].bitcast(U32).indirect(half(lst, 1)))
+            rb = keep.tile([P, W], F32, name=f"rb{a}", tag="h5_early0" if a == 1 else f"rb{a}", align_bytes=64)
+            nc.scalar.activation(pa[:], h[:].indirect(l_n1[:]), COPY)
+            nc.scalar.activation(h5[:], h[:].indirect(l_n5[:, : EARLY // 16]), COPY)
+            nc.vector.tensor_tensor(rb[:], pa[:], pb[:], ALU.max)
+            nc.vector.tensor_scalar(h5g[:], h5[:], gain[:, a : a + 1], None, ALU.mult)
+            nc.scalar.activation(ub[:].indirect(l_n3[:]), pb[:], COPY)
+            nc.scalar.activation(ub[:].indirect(l_n4[:]), rb[:], COPY)
+            if a == 0:
+                nc.vector.tensor_scalar(neg_gain[:], gain[:], -1.0, None, ALU.mult)
+            if a == 1:
+                d_codes, d_plane = d_second, planes_second[:]
+            ubg_tiles.append(ub)
+            h5g_tiles.append(h5g)
+            if a >= 2:
+                done = range(2) if a == 2 else range(2, 3)
+                z_done = keep.tile([P, len(done) * EARLY], BF16, name=f"z_done{a}", tag=f"pa{a}", align_bytes=64)
+                ubg_done = keep.tile([P, len(done) * LATE], F32, name=f"ubg_done{a}", tag=f"h5_early{a}", align_bytes=64)
+                for n, b in enumerate(done):
+                    early_z(b, z_done[:, n * EARLY : (n + 1) * EARLY])
+                    late_gained(b, ubg_done[:, n * LATE : (n + 1) * LATE])
+        z_last = keep.tile([P, EARLY], BF16, name="z_last", align_bytes=64)
+        early_z(PACK - 1, z_last[:])
+
+        def turn_back(zt, grouped, n, name):
+            words = zt.bitcast(F32)
+            back = bank(n, [P, 2, P], F32, name)
+            for u in range(2):
+                nc.tensor.transpose(back[:, u, :], words[:, u : W : 2], ident_f32[:])
+            nc.vector.tensor_copy(grouped.bitcast(F32).rearrange("p (j u) -> p j u", u=2), back[:].rearrange("p u j -> p j u"))
+
+        def second_matmul(acc2, m, codes, plane):
+            nc.tensor.matmul_mx(
+                out=acc2,
+                lhsT=w1_codes[:, 2 * P * m : 2 * P * (m + 1)].bitcast(FP4X4),
+                lhsT_scale=w1_plane[:, P * m : P * (m + 1)],
+                rhs=codes.bitcast(FP8X4),
+                rhs_scale=plane,
+                start=True,
+                stop=True,
+            )
+
+        grouped_early = keep.tile([P, PACK * EARLY], BF16, name="grouped_early", tag="grouped_early", align_bytes=64)
+        turn_back(zt_early[:], grouped_early[:], 4, "back_early")
+        codes_early = keep.tile([P, EARLY], U32, name="codes_early", tag="codes_early", align_bytes=64)
+        plane_early = keep.tile([P, EARLY], U8, name="plane_early", align_bytes=64)
+        nc.vector.quantize_mx(out=codes_early[:].bitcast(FP8X4), scales=plane_early[:], in_=grouped_early[:])
+        h2_early = keep.tile([P, 4, EARLY], F32, name="h2_early")
+        acc_a = bank(5, [P, EARLY], F32, "acc2_early0")
+        second_matmul(acc_a[:], 0, codes_early[:], plane_early[:])
+        nc.vector.tensor_copy(h2_early[:, 0, :], acc_a[:])
+        acc_b = bank(2, [P, 3, EARLY], F32, "acc2_early123")
+        for m in range(1, 4):
+            second_matmul(acc_b[:, m - 1, :], m, codes_early[:], plane_early[:])
+        nc.vector.tensor_copy(h2_early[:, 1:, :], acc_b[:])
+
+        h5_late = keep.tile([P, PACK * LATE], F32, name="h5_late", tag="rb3", align_bytes=64)
+        for a in range(PACK):
+            nc.scalar.activation(h5_late[:, a * LATE : (a + 1) * LATE], h_tiles[a][:].indirect(l_n5[:, EARLY // 16 :]), COPY)
+
+        sent = [[keep.tile([P, S], F32, name=f"sent{m}_{v}") for v in range(2)] for m in range(4)]
+        for m in range(4):
+            for v, lst in enumerate((l_n6, l_n7)):
+                nc.scalar.activation(sent[m][v][:].indirect(lst[:, : EARLY // 16]), h2_early[:, m, :], COPY)
+
+        z_late = keep.tile([P, PACK * LATE], BF16, name="z_late", tag="grouped_early", align_bytes=64)
+        for a in range(PACK):
+            if a == PACK - 1:
+                ubg_last = keep.tile([P, LATE], F32, name="ubg_last", tag="codes_early", align_bytes=64)
+                late_gained(a, ubg_last[:])
+            ubg = gained[a]
+            cols = slice(a * LATE, (a + 1) * LATE)
+            nc.vector.scalar_tensor_tensor(z_late[:, cols], h5_late[:, cols], neg_gain[:, a : a + 1], ubg, ALU.mult, ALU.add)
+            turned = bank(6 + a % 2, [P, 3, P], BF16, f"turned_late{a}")
+            for b in range(3):
+                nc.tensor.transpose(turned[:, b, :], z_late[:, a * LATE + b * P : a * LATE + (b + 1) * P], ident_bf[:])
+            nc.vector.tensor_copy(zt_late[:, :, a * P : (a + 1) * P], turned[:])
+        grouped_late = keep.tile([P, PACK * LATE], BF16, name="grouped_late", align_bytes=64)
+        for b in range(3):
+            turn_back(zt_late[:, b, :], grouped_late[:, b * S : (b + 1) * S], 3 + b, f"back_late{b}")
+        codes_late = keep.tile([P, LATE], U32, name="codes_late", align_bytes=64)
+        plane_late = keep.tile([P, LATE], U8, name="plane_late", align_bytes=64)
+        nc.vector.quantize_mx(out=codes_late[:].bitcast(FP8X4), scales=plane_late[:], in_=grouped_late[:])
+
+        for m in range(4):
+            acc2 = bank(m % 2, [P, LATE], F32, f"acc2_late{m}")
+            for c0, c1 in ((0, W), (W, LATE)):
+                second_matmul(acc2[:, c0:c1], m, codes_late[:, c0:c1], plane_late[:, c0:c1])
+            h2 = keep.tile([P, LATE], F32, name=f"h2_late{m}")
+            nc.vector.tensor_copy(h2[:], acc2[:])
+            for v, lst in enumerate((l_n6, l_n7)):
+                nc.scalar.activation(sent[m][v][:].indirect(lst[:, EARLY // 16 :]), h2[:], COPY)
+            for c in range(2):
+                cols = slice(c * W, (c + 1) * W)
+                res = keep.tile([P, W], F32, name=f"res{m}_{c}")
+                nc.vector.tensor_tensor(res[:], sent[m][0][:, cols], sent[m][1][:, cols], ALU.max)
+                nc.sync.dma_start(out[P * m : P * (m + 1), cols], res[:])

@@ -105,9 +105,9 @@ def tile_picked_mthzncpswsendtwo_none_p_kernel(
         w1_codes = keep.tile([P, 2 * S], U8, name="w1_codes", tag="bytes_first", align_bytes=64)
         nc.sync.dma_start(w1_codes[:].bitcast(I32), w1_words[0].bitcast(I32))
         w1_plane = keep.tile([P, S], U8, name="w1_plane", tag="xw_table", align_bytes=64)
-        nc.gpsimd.memset(w1_plane[:].bitcast(I32), 0)
         for q in range(4):
-            nc.sync.dma_start(w1_plane[32 * q : 32 * q + 4, :].bitcast(I32), w1_scales[0, 4 * q : 4 * q + 4, :].bitcast(I32))
+            rows = w1_scales[0, 4 * q : 4 * q + 4, :].bitcast(I32).unsqueeze(0).to_broadcast([8, 4, S // 4])
+            nc.sync.dma_start(w1_plane[32 * q : 32 * q + 32, :].bitcast(I32), rows)
 
         def first_product(acc, d_codes, d_plane, a, c0, c1):
             for u in range(2):
@@ -126,7 +126,7 @@ def tile_picked_mthzncpswsendtwo_none_p_kernel(
             nc.vector.scalar_tensor_tensor(z, ubg_tiles[a][:, :EARLY], gain[:, a : a + 1], h5g_tiles[a][:], ALU.mult, ALU.subtract)
             turned = bank(3, [P, P], BF16, f"turned_early{a}")
             nc.tensor.transpose(turned[:], z, ident_bf[:])
-            nc.vector.tensor_copy(zt_early[:, a * P : (a + 1) * P], turned[:])
+            nc.vector.tensor_copy(zt_early[:, :, 32 * a : 32 * (a + 1)], turned[:].bitcast(F32).rearrange("j (p u) -> j u p", u=2))
 
         def late_gained(a, ubg):
             nc.vector.tensor_scalar(ubg, ubg_tiles[a][:, EARLY:], gain[:, a : a + 1], None, ALU.mult)
@@ -134,8 +134,8 @@ def tile_picked_mthzncpswsendtwo_none_p_kernel(
 
         h5g_tiles, gained = [], []
         neg_gain = keep.tile([P, PACK], F32, name="neg_gain")
-        zt_early = keep.tile([P, S], BF16, name="zt_early", align_bytes=64)
-        zt_late = keep.tile([P, 3, S], BF16, name="zt_late", align_bytes=64)
+        zt_early = keep.tile([P, 2, P], F32, name="zt_early", align_bytes=64)
+        zt_late = keep.tile([P, 3, 2, P], F32, name="zt_late", align_bytes=64)
         h_tiles, ubg_tiles = [], []
         d_codes, d_plane = d_first, planes_first[:, 2 * S :]
         for a in range(PACK):
@@ -185,10 +185,9 @@ def tile_picked_mthzncpswsendtwo_none_p_kernel(
         early_z(PACK - 1, z_last[:])
 
         def turn_back(zt, grouped, n, name):
-            words = zt.bitcast(F32)
             back = bank(n, [P, 2, P], F32, name)
             for u in range(2):
-                nc.tensor.transpose(back[:, u, :], words[:, u : W : 2], ident_f32[:])
+                nc.tensor.transpose(back[:, u, :], zt[:, u, :], ident_f32[:])
             nc.vector.tensor_copy(grouped.bitcast(F32).rearrange("p (j u) -> p j u", u=2), back[:].rearrange("p u j -> p j u"))
 
         def second_matmul(acc2, m, codes, plane):
@@ -232,17 +231,19 @@ def tile_picked_mthzncpswsendtwo_none_p_kernel(
                 late_gained(a, ubg_last[:])
             ubg = gained[a]
             cols = slice(a * LATE, (a + 1) * LATE)
-            nc.vector.scalar_tensor_tensor(z_late[:, cols], h5_late[:, cols], neg_gain[:, a : a + 1], ubg, ALU.mult, ALU.add)
+            z = z_late[:, cols]
+            nc.vector.scalar_tensor_tensor(z, h5_late[:, cols], neg_gain[:, a : a + 1], ubg, ALU.mult, ALU.add)
             turned = bank(6 + a % 2, [P, 3, P], BF16, f"turned_late{a}")
             for b in range(3):
-                nc.tensor.transpose(turned[:, b, :], z_late[:, a * LATE + b * P : a * LATE + (b + 1) * P], ident_bf[:])
-            nc.vector.tensor_copy(zt_late[:, :, a * P : (a + 1) * P], turned[:])
+                nc.tensor.transpose(turned[:, b, :], z[:, b * P : (b + 1) * P], ident_bf[:])
+            nc.vector.tensor_copy(zt_late[:, :, :, 32 * a : 32 * (a + 1)], turned[:].bitcast(F32).rearrange("j b (p u) -> j b u p", u=2))
         grouped_late = keep.tile([P, PACK * LATE], BF16, name="grouped_late", align_bytes=64)
         for b in range(3):
-            turn_back(zt_late[:, b, :], grouped_late[:, b * S : (b + 1) * S], 3 + b, f"back_late{b}")
+            turn_back(zt_late[:, b], grouped_late[:, b * S : (b + 1) * S], 3 + b, f"back_late{b}")
         codes_late = keep.tile([P, LATE], U32, name="codes_late", align_bytes=64)
         plane_late = keep.tile([P, LATE], U8, name="plane_late", align_bytes=64)
-        nc.vector.quantize_mx(out=codes_late[:].bitcast(FP8X4), scales=plane_late[:], in_=grouped_late[:])
+        for c0, c1 in ((0, W), (W, LATE)):
+            nc.vector.quantize_mx(out=codes_late[:, c0:c1].bitcast(FP8X4), scales=plane_late[:, c0:c1], in_=grouped_late[:, PACK * c0 : PACK * c1])
 
         for m in range(4):
             acc2 = bank(m % 2, [P, LATE], F32, f"acc2_late{m}")

from contextlib import ExitStack

import concourse.mybir as mybir
from concourse.masks import make_identity

F32 = mybir.dt.float32
BF16 = mybir.dt.bfloat16
I32 = mybir.dt.int32
U32 = mybir.dt.uint32
U16 = mybir.dt.uint16
U8 = mybir.dt.uint8
FP8X4 = mybir.dt.float8_e4m3fn_x4
FP4X4 = mybir.dt.float4_e2m1fn_x4
ALU = mybir.AluOpType
COPY = mybir.ActivationFunctionType.Copy

P = 128
PACK = 4
T, G, S, W = 1024, 2048, 512, 256
EARLY = 128
LATE = S - EARLY
FLOPS = 3 * 2 * 512 * 512 * 512


def tile_picked_mthzncpswsendtwo_none_p_kernel(
    tc, x_words, x_scales, d_words, d_scales, gn, w1_words, w1_scales,
    offs, k1, hz, k2, n1, n2, n3, n4, n5, n6, n7, out,
):
    nc = tc.nc
    with ExitStack() as ctx:
        keep = ctx.enter_context(tc.tile_pool(name="keep", bufs=1))
        psum = ctx.enter_context(tc.psum_pool(name="psum", bufs=1))

        def load_list(ap, name):
            tile = keep.tile(list(ap.shape), U16, name=name)
            nc.sync.dma_start(tile[:], ap)
            return tile

        def load_scale_table(ap, cols, name):
            tile = keep.tile([P, cols], U8, name=name, align_bytes=64)
            rows = ap[0].bitcast(I32).unsqueeze(1).to_broadcast([16, 8, cols // 4])
            nc.sync.dma_start(tile[:].bitcast(I32), rows)
            return tile

        def load_word_table(ap, cols, name):
            tile = keep.tile([P, cols], I32, name=name, tag=name, align_bytes=64)
            nc.sync.dma_start(tile[:], ap[0].rearrange("p n t -> p (n t)").bitcast(I32))
            return tile

        l_offs = load_list(offs, "l_offs")
        xs_table = load_scale_table(x_scales, T, "xs_table")
        l_hz = load_list(hz, "l_hz")
        ds_table = load_scale_table(d_scales, G, "ds_table")
        l_k1 = load_list(k1, "l_k1")
        l_k2 = load_list(k2, "l_k2")
        dw_table = load_word_table(d_words, G, "dw_table")
        xw_table = load_word_table(x_words, T, "xw_table")
        l_n1 = load_list(n1, "l_n1")
        l_n2 = load_list(n2, "l_n2")
        l_n5 = load_list(n5, "l_n5")
        l_n3 = load_list(n3, "l_n3")
        l_n4 = load_list(n4, "l_n4")
        l_n6 = load_list(n6, "l_n6")
        l_n7 = load_list(n7, "l_n7")
        gain = keep.tile([P, PACK], F32, name="gain")
        with nc.allow_non_contiguous_dma(reason="one gain a partition and tile"):
            nc.sync.dma_start(gain[:], gn.rearrange("(a p) o -> p (a o)", p=P))
        ident_bf = keep.tile([P, P], BF16, name="ident_bf")
        make_identity(nc, ident_bf[:])
        ident_f32 = keep.tile([P, P], F32, name="ident_f32")
        make_identity(nc, ident_f32[:])

        def bank(n, shape, dtype, name):
            return psum.tile(shape, dtype, name=name, tag=f"bank{n}")

        def place_scale_rows(picked, cols, name):
            plane = keep.tile([P, cols], U8, name=name, tag=name, align_bytes=64)
            nc.vector.memset(plane[:].bitcast(I32), 0)
            for q in range(4):
                nc.sync.dma_start(plane[32 * q : 32 * q + 4, :].bitcast(I32), picked[32 * q : 32 * q + 32 : 8, :].bitcast(I32))
            return plane

        def half(lst, c):
            return lst[:, c * (W // 16) : (c + 1) * (W // 16)]

        bytes_first = keep.tile([P, 3 * S], U8, name="bytes_first", tag="bytes_first", align_bytes=64)
        for u, lst in enumerate((l_offs, l_hz)):
            nc.vector.tensor_copy(bytes_first[:, u * S : (u + 1) * S], xs_table[:].indirect(lst[:]))
        for u, lst in enumerate((l_k1, l_k2)):
            nc.vector.tensor_copy(bytes_first[:, 2 * S + u * W : 2 * S + (u + 1) * W], ds_table[:].indirect(half(lst, 0)))
        planes_first = place_scale_rows(bytes_first, 3 * S, "planes_first")

        d_first = keep.tile([P, S], U32, name="d_first", align_bytes=64)
        x_picked = keep.tile([P, 2 * S], U32, name="x_picked", align_bytes=64)
        for u, lst in enumerate((l_k1, l_k2)):
            nc.vector.tensor_copy(d_first[:, u * W : (u + 1) * W], dw_table[:].bitcast(U32).indirect(half(lst, 0)))
        nc.vector.tensor_copy(x_picked[:, :S], xw_table[:].bitcast(U32).indirect(l_offs[:]))
        for c in range(2):
            nc.vector.tensor_copy(x_picked[:, S + c * W : S + (c + 1) * W], xw_table[:].bitcast(U32).indirect(half(l_hz, c)))

        bytes_second = keep.tile([P, S], U8, name="bytes_second", tag="xw_table", align_bytes=64)
        for u, lst in enumerate((l_k1, l_k2)):
            nc.vector.tensor_copy(bytes_second[:, u * W : (u + 1) * W], ds_table[:].indirect(half(lst, 1)))
        planes_second = place_scale_rows(bytes_second, S, "planes_second")
        w1_codes = keep.tile([P, 2 * S], U8, name="w1_codes", tag="bytes_first", align_bytes=64)
        nc.sync.dma_start(w1_codes[:].bitcast(I32), w1_words[0].bitcast(I32))
        w1_plane = keep.tile([P, S], U8, name="w1_plane", tag="xw_table", align_bytes=64)
        for q in range(4):
            rows = w1_scales[0, 4 * q : 4 * q + 4, :].bitcast(I32).unsqueeze(0).to_broadcast([8, 4, S // 4])
            nc.sync.dma_start(w1_plane[32 * q : 32 * q + 32, :].bitcast(I32), rows)

        def first_product(acc, d_codes, d_plane, a, c0, c1):
            for u in range(2):
                m0 = u * W + (a % 2) * P
                nc.tensor.matmul_mx(
                    out=acc,
                    lhsT=d_codes[:, m0 : m0 + P].bitcast(FP8X4),
                    lhsT_scale=d_plane[:, m0 : m0 + P],
                    rhs=x_picked[:, u * S + c0 : u * S + c1].bitcast(FP8X4),
                    rhs_scale=planes_first[:, u * S + c0 : u * S + c1],
                    start=(u == 0),
                    stop=(u == 1),
                )

        def early_z(a, z):
            nc.vector.scalar_tensor_tensor(z, ubg_tiles[a][:, :EARLY], gain[:, a : a + 1], h5g_tiles[a][:], ALU.mult, ALU.subtract)
            turned = bank(3, [P, P], BF16, f"turned_early{a}")
            nc.tensor.transpose(turned[:], z, ident_bf[:])
            nc.vector.tensor_copy(zt_early[:, :, 32 * a : 32 * (a + 1)], turned[:].bitcast(F32).rearrange("j (p u) -> j u p", u=2))

        def late_gained(a, ubg):
            nc.vector.tensor_scalar(ubg, ubg_tiles[a][:, EARLY:], gain[:, a : a + 1], None, ALU.mult)
            gained.append(ubg)

        h5g_tiles, gained = [], []
        neg_gain = keep.tile([P, PACK], F32, name="neg_gain")
        zt_early = keep.tile([P, 2, P], F32, name="zt_early", align_bytes=64)
        zt_late = keep.tile([P, 3, 2, P], F32, name="zt_late", align_bytes=64)
        h_tiles, ubg_tiles = [], []
        d_codes, d_plane = d_first, planes_first[:, 2 * S :]
        for a in range(PACK):
            h = keep.tile([P, S], F32, name=f"h{a}", tag="pa0" if a == 1 else f"h{a}", align_bytes=64)
            if a == 0:
                for c in range(2):
                    acc = bank(c, [P, W], F32, f"acc0_{c}")
                    first_product(acc[:], d_codes, d_plane, a, c * W, (c + 1) * W)
                    nc.scalar.activation(h[:, c * W : (c + 1) * W], acc[:], COPY, scale=0.0625)
            else:
                acc = bank((a + 1) % 3, [P, S], F32, f"acc{a}")
                first_product(acc[:], d_codes, d_plane, a, 0, S)
                nc.vector.tensor_scalar(h[:], acc[:], 0.0625, None, ALU.mult)
            h_tiles.append(h)

            pa = keep.tile([P, W], F32, name=f"pa{a}", tag=f"pa{a}", align_bytes=64)
            pb = keep.tile([P, W], F32, name=f"pb{a}")
            h5 = keep.tile([P, EARLY], F32, name=f"h5_early{a}", tag=f"h5_early{a}", align_bytes=64)
            h5g = keep.tile([P, EARLY], F32, name=f"h5g_early{a}", tag="planes_second" if a == 1 else f"h5g_early{a}", align_bytes=64)
            ub = keep.tile([P, S], F32, name=f"ub{a}")
            nc.vector.tensor_copy(pb[:], h[:].indirect(l_n2[:]))
            if a == 1:
                d_second = keep.tile([P, S], U32, name="d_second", tag="h5_early0", align_bytes=64)
                for u, lst in enumerate((l_k1, l_k2)):
                    nc.vector.tensor_copy(d_second[:, u * W : (u + 1) * W], dw_table[:].bitcast(U32).indirect(half(lst, 1)))
            rb = keep.tile([P, W], F32, name=f"rb{a}", tag="h5_early0" if a == 1 else f"rb{a}", align_bytes=64)
            nc.scalar.activation(pa[:], h[:].indirect(l_n1[:]), COPY)
            nc.scalar.activation(h5[:], h[:].indirect(l_n5[:, : EARLY // 16]), COPY)
            nc.vector.tensor_tensor(rb[:], pa[:], pb[:], ALU.max)
            nc.vector.tensor_scalar(h5g[:], h5[:], gain[:, a : a + 1], None, ALU.mult)
            nc.scalar.activation(ub[:].indirect(l_n3[:]), pb[:], COPY)
            nc.scalar.activation(ub[:].indirect(l_n4[:]), rb[:], COPY)
            if a == 0:
                nc.vector.tensor_scalar(neg_gain[:], gain[:], -1.0, None, ALU.mult)
            if a == 1:
                d_codes, d_plane = d_second, planes_second[:]
            ubg_tiles.append(ub)
            h5g_tiles.append(h5g)
            if a >= 2:
                done = range(2) if a == 2 else range(2, 3)
                z_done = keep.tile([P, len(done) * EARLY], BF16, name=f"z_done{a}", tag=f"pa{a}", align_bytes=64)
                ubg_done = keep.tile([P, len(done) * LATE], F32, name=f"ubg_done{a}", tag=f"h5_early{a}", align_bytes=64)
                for n, b in enumerate(done):
                    early_z(b, z_done[:, n * EARLY : (n + 1) * EARLY])
                    late_gained(b, ubg_done[:, n * LATE : (n + 1) * LATE])
        z_last = keep.tile([P, EARLY], BF16, name="z_last", align_bytes=64)
        early_z(PACK - 1, z_last[:])

        def turn_back(zt, grouped, n, name):
            back = bank(n, [P, 2, P], F32, name)
            for u in range(2):
                nc.tensor.transpose(back[:, u, :], zt[:, u, :], ident_f32[:])
            nc.vector.tensor_copy(grouped.bitcast(F32).rearrange("p (j u) -> p j u", u=2), back[:].rearrange("p u j -> p j u"))

        def second_matmul(acc2, m, codes, plane):
            nc.tensor.matmul_mx(
                out=acc2,
                lhsT=w1_codes[:, 2 * P * m : 2 * P * (m + 1)].bitcast(FP4X4),
                lhsT_scale=w1_plane[:, P * m : P * (m + 1)],
                rhs=codes.bitcast(FP8X4),
                rhs_scale=plane,
                start=True,
                stop=True,
            )

        grouped_early = keep.tile([P, PACK * EARLY], BF16, name="grouped_early", tag="grouped_early", align_bytes=64)
        turn_back(zt_early[:], grouped_early[:], 4, "back_early")
        codes_early = keep.tile([P, EARLY], U32, name="codes_early", tag="codes_early", align_bytes=64)
        plane_early = keep.tile([P, EARLY], U8, name="plane_early", align_bytes=64)
        nc.vector.quantize_mx(out=codes_early[:].bitcast(FP8X4), scales=plane_early[:], in_=grouped_early[:])
        h2_early = keep.tile([P, 4, EARLY], F32, name="h2_early")
        acc_a = bank(5, [P, EARLY], F32, "acc2_early0")
        second_matmul(acc_a[:], 0, codes_early[:], plane_early[:])
        nc.vector.tensor_copy(h2_early[:, 0, :], acc_a[:])
        acc_b = bank(2, [P, 3, EARLY], F32, "acc2_early123")
        for m in range(1, 4):
            second_matmul(acc_b[:, m - 1, :], m, codes_early[:], plane_early[:])
        nc.vector.tensor_copy(h2_early[:, 1:, :], acc_b[:])

        h5_late = keep.tile([P, PACK * LATE], F32, name="h5_late", tag="rb3", align_bytes=64)
        for a in range(PACK):
            nc.scalar.activation(h5_late[:, a * LATE : (a + 1) * LATE], h_tiles[a][:].indirect(l_n5[:, EARLY // 16 :]), COPY)

        sent = [[keep.tile([P, S], F32, name=f"sent{m}_{v}") for v in range(2)] for m in range(4)]
        for m in range(4):
            for v, lst in enumerate((l_n6, l_n7)):
                nc.scalar.activation(sent[m][v][:].indirect(lst[:, : EARLY // 16]), h2_early[:, m, :], COPY)

        z_late = keep.tile([P, PACK * LATE], BF16, name="z_late", tag="grouped_early", align_bytes=64)
        for a in range(PACK):
            if a == PACK - 1:
                ubg_last = keep.tile([P, LATE], F32, name="ubg_last", tag="codes_early", align_bytes=64)
                late_gained(a, ubg_last[:])
            ubg = gained[a]
            cols = slice(a * LATE, (a + 1) * LATE)
            z = z_late[:, cols]
            nc.vector.scalar_tensor_tensor(z, h5_late[:, cols], neg_gain[:, a : a + 1], ubg, ALU.mult, ALU.add)
            turned = bank(6 + a % 2, [P, 3, P], BF16, f"turned_late{a}")
            for b in range(3):
                nc.tensor.transpose(turned[:, b, :], z[:, b * P : (b + 1) * P], ident_bf[:])
            nc.vector.tensor_copy(zt_late[:, :, :, 32 * a : 32 * (a + 1)], turned[:].bitcast(F32).rearrange("j b (p u) -> j b u p", u=2))
        grouped_late = keep.tile([P, PACK * LATE], BF16, name="grouped_late", align_bytes=64)
        for b in range(3):
            turn_back(zt_late[:, b], grouped_late[:, b * S : (b + 1) * S], 3 + b, f"back_late{b}")
        codes_late = keep.tile([P, LATE], U32, name="codes_late", align_bytes=64)
        plane_late = keep.tile([P, LATE], U8, name="plane_late", align_bytes=64)
        for c0, c1 in ((0, W), (W, LATE)):
            nc.vector.quantize_mx(out=codes_late[:, c0:c1].bitcast(FP8X4), scales=plane_late[:, c0:c1], in_=grouped_late[:, PACK * c0 : PACK * c1])

        for m in range(4):
            acc2 = bank(m % 2, [P, LATE], F32, f"acc2_late{m}")
            for c0, c1 in ((0, W), (W, LATE)):
                second_matmul(acc2[:, c0:c1], m, codes_late[:, c0:c1], plane_late[:, c0:c1])
            h2 = keep.tile([P, LATE], F32, name=f"h2_late{m}")
            nc.vector.tensor_copy(h2[:], acc2[:])
            for v, lst in enumerate((l_n6, l_n7)):
                nc.scalar.activation(sent[m][v][:].indirect(lst[:, EARLY // 16 :]), h2[:], COPY)
            for c in range(2):
                cols = slice(c * W, (c + 1) * W)
                res = keep.tile([P, W], F32, name=f"res{m}_{c}")
                nc.vector.tensor_tensor(res[:], sent[m][0][:, cols], sent[m][1][:, cols], ALU.max)
                nc.sync.dma_start(out[P * m : P * (m + 1), cols], res[:])
